import numpy as np
import ml_dtypes


def mxq(x, axis, fmt="e4m3"):
    dtype, down = {"e4m3": (ml_dtypes.float8_e4m3fn, 7), "e5m2": (ml_dtypes.float8_e5m2, 14)}[fmt]
    v = np.moveaxis(np.asarray(x, np.float32).astype(ml_dtypes.bfloat16).astype(np.float64), axis, -1)
    blocks = v.reshape(v.shape[:-1] + (-1, 32))
    amax = np.abs(blocks).max(-1, keepdims=True)
    byte = np.maximum(np.where(amax > 0, np.frexp(amax)[1] - 1 + 127, 0) - down, 1)
    scale = np.exp2(byte - 127.0)
    codes = (blocks / scale).astype(np.float32).astype(dtype).astype(np.float64)
    return np.moveaxis((codes * scale).reshape(v.shape), -1, axis)


WIDE = False


def mx_kscale(k):
    if not WIDE:
        return np.ones(k)
    levels = np.array([10, -10, 5, -5, 0])
    if k % 512:
        return np.exp2(np.random.permutation(np.resize(levels, k // 32))).repeat(32)
    a = np.empty((k // 512, 16))
    for p in range(k // 512):
        a[p, :8] = np.random.permutation(np.resize(levels, 8))
        for g in range(8):
            far = levels[np.abs(levels - a[p, g]) >= 10]
            a[p, g + 8] = far[np.random.randint(len(far))]
    return np.exp2(a.ravel()).repeat(32)


def f64(x):
    return np.asarray(x).astype(np.float64)


def striped(idx):
    return np.tile(idx.reshape(-1, 16).T, (8, 1)).astype(np.uint16)


def unstriped(offs):
    return offs[:16].T.reshape(-1).astype(np.int64)


def relu(v):
    return np.maximum(v, 0.0)


K, T, D, S, V, H, N = 1536, 1024, 3, 512, 256, 512, 512


def setup_inputs():
    n = np.random.standard_normal
    s = mx_kscale(K)[:, None]
    u = mx_kscale(H)
    return {
        "xT": (n((K, T)) * s).astype(np.float32),
        "w1": (n((K, H)) / np.sqrt(K) / s * u).astype(np.float32),
        "w2": (n((H, N)) / np.sqrt(H) / u[:, None]).astype(np.float32),
        "gate": np.tile(np.random.uniform(0.2, 1.0, (D, 1, V)) / np.sqrt(D), (1, N, 1)).astype(np.float32),
        "offs": striped(np.random.permutation(T)[:S]),
        "pos1": striped(np.random.permutation(S)[:V]),
        "pos2": striped(np.random.permutation(S)[:V]),
        "pos3": striped(np.random.permutation(S)[:V]),
    }


def reference(xT, w1, w2, gate, offs, pos1, pos2, pos3):
    idx = unstriped(offs)
    xq = mxq(f64(xT)[:, idx], 0, "e4m3")
    h = relu(mxq(f64(w1), 0, "e4m3").T @ xq)
    y = mxq(f64(w2), 0, "e4m3").T @ mxq(h, 0, "e4m3")
    return sum(f64(gate[d]) * y[:, unstriped(p)] for d, p in enumerate((pos1, pos2, pos3)))

@@ -1,0 +1,227 @@
+from contextlib import ExitStack
+
+import concourse.mybir as mybir
+from concourse.masks import make_identity
+
+K, T, D, S, V, H, N = 1536, 1024, 3, 512, 256, 512, 512
+P = 128
+PACK = 4
+KP = P * PACK
+PASSES = K // KP
+NB = N // P
+CH = 128
+NCH = S // CH
+FLOPS = 2 * S * H * (K + N) + 5 * N * V
+
+F32 = mybir.dt.float32
+BF16 = mybir.dt.bfloat16
+U32 = mybir.dt.uint32
+U16 = mybir.dt.uint16
+U8 = mybir.dt.uint8
+FP8X4 = mybir.dt.float8_e4m3fn_x4
+RELU = mybir.ActivationFunctionType.Relu
+MULT = mybir.AluOpType.mult
+ADD = mybir.AluOpType.add
+
+X_VEC = 384
+W1_VEC = 48
+
+
+def tile_picked_sub_mlp_relu_sub_e_kernel(tc, xT, w1, w2, gate, offs, pos1, pos2, pos3, out):
+    nc = tc.nc
+    with ExitStack() as ctx:
+        keep = ctx.enter_context(tc.tile_pool(name="keep", bufs=1))
+        psum = ctx.enter_context(tc.psum_pool(name="psum", bufs=1))
+
+        def tile(shape, dtype, name):
+            return keep.tile(shape, dtype, name=name, align_bytes=64)
+
+        offs_sb = tile([P, S // 16], U16, "offs_sb")
+        pos_sb = [tile([P, V // 16], U16, "pos_sb%d" % d) for d in range(D)]
+        x_raw = [[tile([P, 2, T], F32, "x_raw%d%d" % (s, u)) for u in range(2)] for s in range(PASSES)]
+        x_pair = [[tile([P, 2 * T], BF16, "x_pair%d%d" % (s, u)) for u in range(2)] for s in range(PASSES)]
+        x_pick = [tile([P, PACK * S], BF16, "x_pick%d" % s) for s in range(PASSES)]
+        x_codes = [tile([P, S], U32, "x_codes%d" % s) for s in range(PASSES)]
+        x_scales = [tile([P, S], U8, "x_scales%d" % s) for s in range(PASSES)]
+        w1_raw = [tile([P, PACK, H], F32, "w1_raw%d" % s) for s in range(PASSES)]
+        w1_grp = [tile([P, PACK * H], BF16, "w1_grp%d" % s) for s in range(PASSES)]
+        w1_codes = [tile([P, H], U32, "w1_codes%d" % s) for s in range(PASSES)]
+        w1_scales = [tile([P, H], U8, "w1_scales%d" % s) for s in range(PASSES)]
+        w2_raw = tile([P, PACK, N], F32, "w2_raw")
+        w2_grp = tile([P, PACK * N], BF16, "w2_grp")
+        w2_codes = tile([P, N], U32, "w2_codes")
+        w2_scales = tile([P, N], U8, "w2_scales")
+        h_grp = [tile([P, PACK * CH], BF16, "h_grp%d" % c) for c in range(NCH)]
+        h_codes = tile([P, S], U32, "h_codes")
+        h_scales = tile([P, S], U8, "h_scales")
+        y_sb = [tile([P, S], F32, "y_sb%d" % m) for m in range(NB)]
+        gate_sb = [tile([P, D, V], F32, "gate_sb%d" % m) for m in range(NB)]
+        prod = [[tile([P, V], F32, "prod%d%d" % (m, d)) for d in range(D)] for m in range(NB)]
+        part = [tile([P, V], F32, "part%d" % m) for m in range(NB)]
+        res = [tile([P, V], F32, "res%d" % m) for m in range(NB)]
+        h_ps = [psum.tile([P, PACK, CH], F32, name="h_ps%d" % c) for c in range(NCH)]
+        warm_ps = psum.tile([P, PACK, P], BF16, name="warm_ps", tag="y_ps3")
+        ident = tile([P, P], BF16, "ident")
+        make_identity(nc, ident[:])
+
+        def load_x(s, u, t0, t1):
+            rows = xT[s * KP : (s + 1) * KP, :].rearrange("(p u e) t -> p u e t", u=2, e=2)
+            nc.sync.dma_start(out=x_raw[s][u][:, :, t0:t1], in_=rows[:, u, :, t0:t1])
+
+        def load_w1(s):
+            nc.sync.dma_start(out=w1_raw[s][:], in_=w1[s * KP : (s + 1) * KP, :].rearrange("(p j) h -> p j h", j=PACK))
+
+        def pair_x(copy, s, u, t0, t1):
+            copy(
+                out=x_pair[s][u][:, 2 * t0 : 2 * t1].rearrange("p (t e) -> p t e", e=2),
+                in_=x_raw[s][u][:, :, t0:t1].rearrange("p e t -> p t e"),
+            )
+
+        def group_w1(copy, s, m0, m1):
+            copy(
+                out=w1_grp[s][:].rearrange("p (t m j) -> p m t j", t=4, j=PACK)[:, m0:m1],
+                in_=w1_raw[s][:].rearrange("p j (m t) -> p m t j", t=4)[:, m0:m1],
+            )
+
+        def group_w2(copy, n0, n1):
+            copy(
+                out=w2_grp[:, PACK * n0 : PACK * n1].rearrange("p (n j) -> p n j", j=PACK),
+                in_=w2_raw[:, :, n0:n1].rearrange("p j n -> p n j"),
+            )
+
+        def pick_x(s, u, n0, n1):
+            words = x_pick[s][:].bitcast(U32).rearrange("p (n u) -> p n u", u=2)
+            nc.vector.tensor_copy(words[:, n0:n1, u], x_pair[s][u][:].bitcast(U32).indirect(offs_sb[:, n0 // 16 : n1 // 16]))
+
+        def quantize(codes, scales, grouped, n0, n1):
+            nc.vector.quantize_mx(
+                out=codes[:, n0:n1].bitcast(FP8X4), scales=scales[:, n0:n1], in_=grouped[:, PACK * n0 : PACK * n1]
+            )
+
+        def first_layer(s, c, t):
+            nc.tensor.matmul_mx(
+                out=h_ps[c][:, t, :],
+                lhsT=w1_codes[s][:, t * P : (t + 1) * P].bitcast(FP8X4),
+                lhsT_scale=w1_scales[s][:, t * P : (t + 1) * P],
+                rhs=x_codes[s][:, c * CH : (c + 1) * CH].bitcast(FP8X4),
+                rhs_scale=x_scales[s][:, c * CH : (c + 1) * CH],
+                start=(s == 0),
+                stop=(s == PASSES - 1),
+            )
+
+        def warm(s, u, b):
+            nc.tensor.transpose(warm_ps[:, b % PACK, :], x_pair[s][u][:, b * P : (b + 1) * P], ident[:])
+
+        def pool(out, in_):
+            nc.gpsimd.tensor_scalar(out=out, in0=in_, scalar1=1.0, scalar2=0.0, op0=MULT, op1=ADD)
+
+        vec, act = nc.vector.tensor_copy, nc.scalar.copy
+
+        load_x(0, 0, 0, T)
+        nc.sync.dma_start(offs_sb[:], offs)
+        load_x(0, 1, 0, T)
+        load_w1(0)
+        load_x(1, 0, 0, T)
+        load_x(1, 1, 0, T)
+        load_w1(1)
+        load_w1(2)
+        load_x(2, 0, 0, T)
+        load_x(2, 1, 0, T // 2)
+        load_x(2, 1, T // 2, T)
+        w2_rows = w2.rearrange("(p j) n -> p j n", j=PACK)
+        for n0 in (0, N // 2):
+            nc.sync.dma_start(out=w2_raw[:, :, n0 : n0 + N // 2], in_=w2_rows[:, :, n0 : n0 + N // 2])
+        for d, pos in enumerate((pos1, pos2, pos3)):
+            nc.sync.dma_start(pos_sb[d][:], pos)
+        for m in range(NB):
+            nc.sync.dma_start(out=gate_sb[m][:], in_=gate[:, m * P : (m + 1) * P, :].rearrange("d p v -> p d v"))
+
+        def do_w1(s):
+            group_w1(act, s, W1_VEC, P)
+            group_w1(vec, s, 0, W1_VEC)
+            quantize(w1_codes[s], w1_scales[s], w1_grp[s], 0, H)
+
+        def do_x(s, u):
+            pair_x(act, s, u, X_VEC, T)
+            pair_x(vec, s, u, 0, X_VEC)
+            pick_x(s, u, 0, S)
+
+        for s in range(2):
+            do_x(s, 0)
+            do_x(s, 1)
+            quantize(x_codes[s], x_scales[s], x_pick[s], 0, S)
+            do_w1(s)
+            for c in range(NCH):
+                first_layer(s, c, 0)
+        do_w1(2)
+        pair_x(act, 2, 0, 640, T)
+        pair_x(vec, 2, 0, 0, 640)
+        pick_x(2, 0, 0, S)
+        pair_x(act, 2, 1, 0, T // 2)
+        pair_x(vec, 2, 1, T // 2, 832)
+        pair_x(act, 2, 1, 832, T)
+        for b in range(32):
+            warm(2, 0, b % 16)
+        for b in range(16):
+            warm(2, 1, b)
+        pick_x(2, 1, 0, 128)
+        pick_x(2, 1, 128, 256)
+        quantize(x_codes[2], x_scales[2], x_pick[2], 0, 128)
+        pick_x(2, 1, 256, 512)
+        quantize(x_codes[2], x_scales[2], x_pick[2], 128, 256)
+        quantize(x_codes[2], x_scales[2], x_pick[2], 256, 512)
+        for q in range(2):
+            group_w2(act, q * P, (q + 1) * P)
+        for q in range(2, 4):
+            group_w2(pool, q * P, (q + 1) * P)
+        for c in range(NCH):
+            first_layer(2, c, 0)
+            for t in range(1, PACK):
+                for s in range(PASSES):
+                    first_layer(s, c, t)
+            nc.scalar.activation(h_grp[c][:].rearrange("p (n t) -> p n t", t=PACK), h_ps[c][:].rearrange("p t n -> p n t"), RELU)
+            if c == 2:
+                quantize(w2_codes, w2_scales, w2_grp, 0, P)
+            nc.vector.quantize_mx(
+                out=h_codes[:, c * CH : (c + 1) * CH].bitcast(FP8X4), scales=h_scales[:, c * CH : (c + 1) * CH], in_=h_grp[c][:]
+            )
+
+        y_ps = [psum.tile([P, S], F32, name="y_ps%d" % m) for m in range(NB)]
+        y_ps_late = psum.tile([P, S], F32, name="y_ps_late", tag="h_ps0")
+
+        def second_layer(bank, m, n0, n1):
+            cols = slice(m * P, (m + 1) * P)
+            nc.tensor.matmul_mx(
+                out=bank[:, n0:n1],
+                lhsT=w2_codes[:, cols].bitcast(FP8X4),
+                lhsT_scale=w2_scales[:, cols],
+                rhs=h_codes[:, n0:n1].bitcast(FP8X4),
+                rhs_scale=h_scales[:, n0:n1],
+                start=True,
+                stop=True,
+            )
+
+        second_layer(y_ps[0], 0, 0, S // 2)
+        nc.scalar.copy(y_sb[0][:, : S // 2], y_ps[0][:, : S // 2])
+        second_layer(y_ps_late, 0, S // 2, S)
+        nc.scalar.copy(y_sb[0][:, S // 2 :], y_ps_late[:, S // 2 :])
+        for m in range(1, NB):
+            quantize(w2_codes, w2_scales, w2_grp, m * P, (m + 1) * P)
+        for m in range(1, NB):
+            second_layer(y_ps[m], m, 0, S)
+            nc.scalar.copy(y_sb[m][:], y_ps[m][:])
+        def add_parts(m):
+            nc.vector.tensor_tensor(part[m][:], prod[m][0][:], prod[m][1][:], ADD)
+
+        def add_last(m):
+            nc.vector.tensor_tensor(res[m][:], part[m][:], prod[m][2][:], ADD)
+            nc.sync.dma_start(out=out[m * P : (m + 1) * P, :], in_=res[m][:])
+
+        for m in range(NB):
+            for d in range(D):
+                nc.vector.tensor_tensor(prod[m][d][:], y_sb[m][:].indirect(pos_sb[d][:]), gate_sb[m][:, d, :], MULT)
+                if m and d == 0:
+                    add_last(m - 1)
+                if d == 2:
+                    add_parts(m)
+        add_last(NB - 1)

@@ -1,7 +1,6 @@
 from contextlib import ExitStack
 
 import concourse.mybir as mybir
-from concourse.masks import make_identity
 
 K, T, D, S, V, H, N = 1536, 1024, 3, 512, 256, 512, 512
 P = 128
@@ -23,8 +22,7 @@ RELU = mybir.ActivationFunctionType.Relu
 MULT = mybir.AluOpType.mult
 ADD = mybir.AluOpType.add
 
-X_VEC = 384
-W1_VEC = 48
+WARM = 12
 
 
 def tile_picked_sub_mlp_relu_sub_e_kernel(tc, xT, w1, w2, gate, offs, pos1, pos2, pos3, out):
@@ -38,16 +36,24 @@ def tile_picked_sub_mlp_relu_sub_e_kernel(tc, xT, w1, w2, gate, offs, pos1, pos2
 
         offs_sb = tile([P, S // 16], U16, "offs_sb")
         pos_sb = [tile([P, V // 16], U16, "pos_sb%d" % d) for d in range(D)]
-        x_raw = [[tile([P, 2, T], F32, "x_raw%d%d" % (s, u)) for u in range(2)] for s in range(PASSES)]
-        x_pair = [[tile([P, 2 * T], BF16, "x_pair%d%d" % (s, u)) for u in range(2)] for s in range(PASSES)]
-        x_pick = [tile([P, PACK * S], BF16, "x_pick%d" % s) for s in range(PASSES)]
+        x_cuts = (((0, 256), (256, 512), (512, T)), ((0, 512), (512, T)), ((0, 512), (512, T)))
+        x_raw = {
+            (s, cut): tile([P, PACK, cut[1] - cut[0]], F32, "x_raw%d_%d" % (s, cut[0])) for s in range(PASSES) for cut in x_cuts[s]
+        }
+        x_grp = [tile([P, PACK * T], BF16, "x_grp%d" % s) for s in range(PASSES)]
+        x_all = [tile([P, T], U32, "x_all%d" % s) for s in range(PASSES)]
+        x_all_sc = tile([P, T], U8, "x_all_sc")
         x_codes = [tile([P, S], U32, "x_codes%d" % s) for s in range(PASSES)]
-        x_scales = [tile([P, S], U8, "x_scales%d" % s) for s in range(PASSES)]
-        w1_raw = [tile([P, PACK, H], F32, "w1_raw%d" % s) for s in range(PASSES)]
+        x_scales = tile([P, S], U8, "x_scales")
+        w1_cuts = ((0, H),), ((0, H),), ((0, H // 2), (H // 2, H))
+        w1_raw = {
+            (s, cut): tile([P, PACK, cut[1] - cut[0]], F32, "w1_raw%d_%d" % (s, cut[0])) for s in range(PASSES) for cut in w1_cuts[s]
+        }
         w1_grp = [tile([P, PACK * H], BF16, "w1_grp%d" % s) for s in range(PASSES)]
         w1_codes = [tile([P, H], U32, "w1_codes%d" % s) for s in range(PASSES)]
         w1_scales = [tile([P, H], U8, "w1_scales%d" % s) for s in range(PASSES)]
-        w2_raw = tile([P, PACK, N], F32, "w2_raw")
+        w2_cuts = ((0, N // 2), (N // 2, N))
+        w2_raw = {cut: tile([P, PACK, N // 2], F32, "w2_raw%d" % cut[0]) for cut in w2_cuts}
         w2_grp = tile([P, PACK * N], BF16, "w2_grp")
         w2_codes = tile([P, N], U32, "w2_codes")
         w2_scales = tile([P, N], U8, "w2_scales")
@@ -60,128 +66,121 @@ def tile_picked_sub_mlp_relu_sub_e_kernel(tc, xT, w1, w2, gate, offs, pos1, pos2
         part = [tile([P, V], F32, "part%d" % m) for m in range(NB)]
         res = [tile([P, V], F32, "res%d" % m) for m in range(NB)]
         h_ps = [psum.tile([P, PACK, CH], F32, name="h_ps%d" % c) for c in range(NCH)]
-        warm_ps = psum.tile([P, PACK, P], BF16, name="warm_ps", tag="y_ps3")
-        ident = tile([P, P], BF16, "ident")
-        make_identity(nc, ident[:])
 
-        def load_x(s, u, t0, t1):
-            rows = xT[s * KP : (s + 1) * KP, :].rearrange("(p u e) t -> p u e t", u=2, e=2)
-            nc.sync.dma_start(out=x_raw[s][u][:, :, t0:t1], in_=rows[:, u, :, t0:t1])
+        def load_x(s, cut):
+            rows = xT[s * KP : (s + 1) * KP, cut[0] : cut[1]].rearrange("(p j) t -> p j t", j=PACK)
+            nc.sync.dma_start(out=x_raw[s, cut][:], in_=rows)
 
-        def load_w1(s):
-            nc.sync.dma_start(out=w1_raw[s][:], in_=w1[s * KP : (s + 1) * KP, :].rearrange("(p j) h -> p j h", j=PACK))
+        def load_w1(s, cut):
+            rows = w1[s * KP : (s + 1) * KP, cut[0] : cut[1]].rearrange("(p j) h -> p j h", j=PACK)
+            nc.sync.dma_start(out=w1_raw[s, cut][:], in_=rows)
 
-        def pair_x(copy, s, u, t0, t1):
+        def group(copy, grp, g0, raw, r0, r1):
             copy(
-                out=x_pair[s][u][:, 2 * t0 : 2 * t1].rearrange("p (t e) -> p t e", e=2),
-                in_=x_raw[s][u][:, :, t0:t1].rearrange("p e t -> p t e"),
+                out=grp[:, PACK * (g0 + r0) : PACK * (g0 + r1)].rearrange("p (c i j) -> p c j i", i=4, j=PACK),
+                in_=raw[:, :, r0:r1].rearrange("p j (c i) -> p c j i", i=4),
             )
 
-        def group_w1(copy, s, m0, m1):
+        def group_w1(copy, s, cut):
             copy(
-                out=w1_grp[s][:].rearrange("p (t m j) -> p m t j", t=4, j=PACK)[:, m0:m1],
-                in_=w1_raw[s][:].rearrange("p j (m t) -> p m t j", t=4)[:, m0:m1],
+                out=w1_grp[s][:].rearrange("p (t m j) -> p m j t", t=4, j=PACK)[:, cut[0] // 4 : cut[1] // 4],
+                in_=w1_raw[s, cut][:].rearrange("p j (m t) -> p m j t", t=4),
             )
-
-        def group_w2(copy, n0, n1):
-            copy(
-                out=w2_grp[:, PACK * n0 : PACK * n1].rearrange("p (n j) -> p n j", j=PACK),
-                in_=w2_raw[:, :, n0:n1].rearrange("p j n -> p n j"),
-            )
-
-        def pick_x(s, u, n0, n1):
-            words = x_pick[s][:].bitcast(U32).rearrange("p (n u) -> p n u", u=2)
-            nc.vector.tensor_copy(words[:, n0:n1, u], x_pair[s][u][:].bitcast(U32).indirect(offs_sb[:, n0 // 16 : n1 // 16]))
 
         def quantize(codes, scales, grouped, n0, n1):
             nc.vector.quantize_mx(
                 out=codes[:, n0:n1].bitcast(FP8X4), scales=scales[:, n0:n1], in_=grouped[:, PACK * n0 : PACK * n1]
             )
 
-        def first_layer(s, c, t):
-            nc.tensor.matmul_mx(
-                out=h_ps[c][:, t, :],
-                lhsT=w1_codes[s][:, t * P : (t + 1) * P].bitcast(FP8X4),
-                lhsT_scale=w1_scales[s][:, t * P : (t + 1) * P],
-                rhs=x_codes[s][:, c * CH : (c + 1) * CH].bitcast(FP8X4),
-                rhs_scale=x_scales[s][:, c * CH : (c + 1) * CH],
-                start=(s == 0),
-                stop=(s == PASSES - 1),
+        def do_x(s, cut, share):
+            width = cut[1] - cut[0]
+            n_act = int(width * share) // 8 * 8
+            if n_act:
+                group(act, x_grp[s], cut[0], x_raw[s, cut], 0, n_act)
+            if n_act < width:
+                group(vec, x_grp[s], cut[0], x_raw[s, cut], n_act, width)
+            quantize(x_all[s], x_all_sc[PACK * s :, :], x_grp[s], cut[0], cut[1])
+
+        def pick_words(s, c0, c1):
+            nc.vector.tensor_copy(
+                x_codes[s][:, c0 * CH : c1 * CH], x_all[s][:].indirect(offs_sb[:, c0 * CH // 16 : c1 * CH // 16])
             )
 
-        def warm(s, u, b):
-            nc.tensor.transpose(warm_ps[:, b % PACK, :], x_pair[s][u][:, b * P : (b + 1) * P], ident[:])
+        def pick_bytes(c0, c1):
+            nc.vector.tensor_copy(
+                x_scales[:, c0 * CH : c1 * CH], x_all_sc[:].indirect(offs_sb[:, c0 * CH // 16 : c1 * CH // 16])
+            )
 
-        def pool(out, in_):
-            nc.gpsimd.tensor_scalar(out=out, in0=in_, scalar1=1.0, scalar2=0.0, op0=MULT, op1=ADD)
+        def first_layer(s, c, t, start, stop, ts=None):
+            nc.tensor.matmul_mx(
+                out=h_ps[c][:, t, :],
+                lhsT=w1_codes[s][:, (ts or t) * P : ((ts or t) + 1) * P].bitcast(FP8X4),
+                lhsT_scale=w1_scales[s][:, (ts or t) * P : ((ts or t) + 1) * P],
+                rhs=x_codes[s][:, c * CH : (c + 1) * CH].bitcast(FP8X4),
+                rhs_scale=x_scales[PACK * s :, c * CH : (c + 1) * CH],
+                start=start,
+                stop=stop,
+            )
 
         vec, act = nc.vector.tensor_copy, nc.scalar.copy
 
-        load_x(0, 0, 0, T)
+        load_x(0, x_cuts[0][0])
         nc.sync.dma_start(offs_sb[:], offs)
-        load_x(0, 1, 0, T)
-        load_w1(0)
-        load_x(1, 0, 0, T)
-        load_x(1, 1, 0, T)
-        load_w1(1)
-        load_w1(2)
-        load_x(2, 0, 0, T)
-        load_x(2, 1, 0, T // 2)
-        load_x(2, 1, T // 2, T)
-        w2_rows = w2.rearrange("(p j) n -> p j n", j=PACK)
-        for n0 in (0, N // 2):
-            nc.sync.dma_start(out=w2_raw[:, :, n0 : n0 + N // 2], in_=w2_rows[:, :, n0 : n0 + N // 2])
+        load_x(0, x_cuts[0][1])
+        load_x(0, x_cuts[0][2])
+        load_w1(0, w1_cuts[0][0])
+        load_x(1, x_cuts[1][0])
+        load_x(1, x_cuts[1][1])
+        load_x(2, x_cuts[2][0])
+        load_x(2, x_cuts[2][1])
+        load_w1(1, w1_cuts[1][0])
+        load_w1(2, w1_cuts[2][0])
+        load_w1(2, w1_cuts[2][1])
+        for cut in w2_cuts:
+            nc.sync.dma_start(out=w2_raw[cut][:], in_=w2[:, cut[0] : cut[1]].rearrange("(p j) n -> p j n", j=PACK))
         for d, pos in enumerate((pos1, pos2, pos3)):
             nc.sync.dma_start(pos_sb[d][:], pos)
         for m in range(NB):
             nc.sync.dma_start(out=gate_sb[m][:], in_=gate[:, m * P : (m + 1) * P, :].rearrange("d p v -> p d v"))
 
-        def do_w1(s):
-            group_w1(act, s, W1_VEC, P)
-            group_w1(vec, s, 0, W1_VEC)
+        def do_w1(s, copy):
+            group_w1(copy, s, w1_cuts[s][0])
             quantize(w1_codes[s], w1_scales[s], w1_grp[s], 0, H)
 
-        def do_x(s, u):
-            pair_x(act, s, u, X_VEC, T)
-            pair_x(vec, s, u, 0, X_VEC)
-            pick_x(s, u, 0, S)
-
-        for s in range(2):
-            do_x(s, 0)
-            do_x(s, 1)
-            quantize(x_codes[s], x_scales[s], x_pick[s], 0, S)
-            do_w1(s)
-            for c in range(NCH):
-                first_layer(s, c, 0)
-        do_w1(2)
-        pair_x(act, 2, 0, 640, T)
-        pair_x(vec, 2, 0, 0, 640)
-        pick_x(2, 0, 0, S)
-        pair_x(act, 2, 1, 0, T // 2)
-        pair_x(vec, 2, 1, T // 2, 832)
-        pair_x(act, 2, 1, 832, T)
-        for b in range(32):
-            warm(2, 0, b % 16)
-        for b in range(16):
-            warm(2, 1, b)
-        pick_x(2, 1, 0, 128)
-        pick_x(2, 1, 128, 256)
-        quantize(x_codes[2], x_scales[2], x_pick[2], 0, 128)
-        pick_x(2, 1, 256, 512)
-        quantize(x_codes[2], x_scales[2], x_pick[2], 128, 256)
-        quantize(x_codes[2], x_scales[2], x_pick[2], 256, 512)
-        for q in range(2):
-            group_w2(act, q * P, (q + 1) * P)
-        for q in range(2, 4):
-            group_w2(pool, q * P, (q + 1) * P)
+        do_x(0, x_cuts[0][0], 0.5)
+        do_x(0, x_cuts[0][1], 0.5)
+        do_x(0, x_cuts[0][2], 0.45)
+        pick_words(0, 0, NCH)
+        do_w1(0, act)
+        do_x(1, x_cuts[1][0], 0.4)
+        do_x(1, x_cuts[1][1], 0.6)
+        pick_words(1, 0, NCH)
+        do_x(2, x_cuts[2][0], 0.6)
+        do_x(2, x_cuts[2][1], 0.5)
         for c in range(NCH):
-            first_layer(2, c, 0)
+            pick_bytes(c, c + 1)
+            pick_words(2, c, c + 1)
+        for b in range(WARM):
+            first_layer(0, b % NCH, 0, True, True, ts=1 + b % 3)
+        for c in range(NCH):
+            first_layer(0, c, 0, True, False)
+        do_w1(1, act)
+        for c in range(NCH):
+            first_layer(1, c, 0, False, False)
+        group_w1(act, 2, w1_cuts[2][0])
+        group_w1(vec, 2, w1_cuts[2][1])
+        for t in range(PACK):
+            quantize(w1_codes[2], w1_scales[2], w1_grp[2], t * P, (t + 1) * P)
+        group(vec, w2_grp, 0, w2_raw[w2_cuts[0]], 0, N // 2)
+        for c in range(NCH):
+            first_layer(2, c, 0, False, True)
             for t in range(1, PACK):
                 for s in range(PASSES):
-                    first_layer(s, c, t)
+                    first_layer(s, c, t, s == 0, s == PASSES - 1)
             nc.scalar.activation(h_grp[c][:].rearrange("p (n t) -> p n t", t=PACK), h_ps[c][:].rearrange("p t n -> p n t"), RELU)
-            if c == 2:
-                quantize(w2_codes, w2_scales, w2_grp, 0, P)
+            if c == 0:
+                group(vec, w2_grp, N // 2, w2_raw[w2_cuts[1]], 0, N // 2)
+                quantize(w2_codes, w2_scales, w2_grp, 0, N)
             nc.vector.quantize_mx(
                 out=h_codes[:, c * CH : (c + 1) * CH].bitcast(FP8X4), scales=h_scales[:, c * CH : (c + 1) * CH], in_=h_grp[c][:]
             )
@@ -206,10 +205,9 @@ def tile_picked_sub_mlp_relu_sub_e_kernel(tc, xT, w1, w2, gate, offs, pos1, pos2
         second_layer(y_ps_late, 0, S // 2, S)
         nc.scalar.copy(y_sb[0][:, S // 2 :], y_ps_late[:, S // 2 :])
         for m in range(1, NB):
-            quantize(w2_codes, w2_scales, w2_grp, m * P, (m + 1) * P)
-        for m in range(1, NB):
             second_layer(y_ps[m], m, 0, S)
             nc.scalar.copy(y_sb[m][:], y_ps[m][:])
+
         def add_parts(m):
             nc.vector.tensor_tensor(part[m][:], prod[m][0][:], prod[m][1][:], ADD)
 

@@ -8,8 +8,8 @@ PACK = 4
 KP = P * PACK
 PASSES = K // KP
 NB = N // P
-CH = 128
-NCH = S // CH
+HALF = S // 2
+WARM = 6
 FLOPS = 2 * S * H * (K + N) + 5 * N * V
 
 F32 = mybir.dt.float32
@@ -21,8 +21,6 @@ FP8X4 = mybir.dt.float8_e4m3fn_x4
 RELU = mybir.ActivationFunctionType.Relu
 MULT = mybir.AluOpType.mult
 ADD = mybir.AluOpType.add
-
-WARM = 12
 
 
 def tile_picked_sub_mlp_relu_sub_e_kernel(tc, xT, w1, w2, gate, offs, pos1, pos2, pos3, out):
@@ -54,10 +52,10 @@ def tile_picked_sub_mlp_relu_sub_e_kernel(tc, xT, w1, w2, gate, offs, pos1, pos2
         w1_scales = [tile([P, H], U8, "w1_scales%d" % s) for s in range(PASSES)]
         w2_cuts = ((0, N // 2), (N // 2, N))
         w2_raw = {cut: tile([P, PACK, N // 2], F32, "w2_raw%d" % cut[0]) for cut in w2_cuts}
-        w2_grp = tile([P, PACK * N], BF16, "w2_grp")
         w2_codes = tile([P, N], U32, "w2_codes")
         w2_scales = tile([P, N], U8, "w2_scales")
-        h_grp = [tile([P, PACK * CH], BF16, "h_grp%d" % c) for c in range(NCH)]
+        h_lin = [tile([P, PACK, HALF], BF16, "h_lin%d" % g) for g in range(2)]
+        h_grp = [tile([P, PACK * HALF], BF16, "h_grp%d" % g) for g in range(2)]
         h_codes = tile([P, S], U32, "h_codes")
         h_scales = tile([P, S], U8, "h_scales")
         y_sb = [tile([P, S], F32, "y_sb%d" % m) for m in range(NB)]
@@ -65,7 +63,7 @@ def tile_picked_sub_mlp_relu_sub_e_kernel(tc, xT, w1, w2, gate, offs, pos1, pos2
         prod = [[tile([P, V], F32, "prod%d%d" % (m, d)) for d in range(D)] for m in range(NB)]
         part = [tile([P, V], F32, "part%d" % m) for m in range(NB)]
         res = [tile([P, V], F32, "res%d" % m) for m in range(NB)]
-        h_ps = [psum.tile([P, PACK, CH], F32, name="h_ps%d" % c) for c in range(NCH)]
+        h_ps = [[psum.tile([P, HALF], F32, name="h_ps%d%d" % (t, g)) for g in range(2)] for t in range(PACK)]
 
         def load_x(s, cut):
             rows = xT[s * KP : (s + 1) * KP, cut[0] : cut[1]].rearrange("(p j) t -> p j t", j=PACK)
@@ -81,10 +79,15 @@ def tile_picked_sub_mlp_relu_sub_e_kernel(tc, xT, w1, w2, gate, offs, pos1, pos2
                 in_=raw[:, :, r0:r1].rearrange("p j (c i) -> p c j i", i=4),
             )
 
-        def group_w1(copy, s, cut):
+        def group_w1(copy, s, cut, t0, t1):
             copy(
-                out=w1_grp[s][:].rearrange("p (t m j) -> p m j t", t=4, j=PACK)[:, cut[0] // 4 : cut[1] // 4],
-                in_=w1_raw[s, cut][:].rearrange("p j (m t) -> p m j t", t=4),
+                out=w1_grp[s][:].rearrange("p (t m j) -> p m j t", t=4, j=PACK)[:, cut[0] // 4 : cut[1] // 4, :, t0:t1],
+                in_=w1_raw[s, cut][:].rearrange("p j (m t) -> p m j t", t=4)[:, :, :, t0:t1],
+            )
+
+        def quantize_w2(m):
+            nc.vector.quantize_mx(
+                out=w2_codes[:, m * P : (m + 1) * P].bitcast(FP8X4), scales=w2_scales[:, m * P : (m + 1) * P], in_=w2_grp[m][:]
             )
 
         def quantize(codes, scales, grouped, n0, n1):
@@ -101,26 +104,26 @@ def tile_picked_sub_mlp_relu_sub_e_kernel(tc, xT, w1, w2, gate, offs, pos1, pos2
                 group(vec, x_grp[s], cut[0], x_raw[s, cut], n_act, width)
             quantize(x_all[s], x_all_sc[PACK * s :, :], x_grp[s], cut[0], cut[1])
 
-        def pick_words(s, c0, c1):
-            nc.vector.tensor_copy(
-                x_codes[s][:, c0 * CH : c1 * CH], x_all[s][:].indirect(offs_sb[:, c0 * CH // 16 : c1 * CH // 16])
-            )
+        def pick_words(s):
+            nc.vector.tensor_copy(x_codes[s][:], x_all[s][:].indirect(offs_sb[:]))
 
-        def pick_bytes(c0, c1):
-            nc.vector.tensor_copy(
-                x_scales[:, c0 * CH : c1 * CH], x_all_sc[:].indirect(offs_sb[:, c0 * CH // 16 : c1 * CH // 16])
-            )
-
-        def first_layer(s, c, t, start, stop, ts=None):
+        def first_layer(s, t, g):
+            cols = slice(t * P, (t + 1) * P)
+            tokens = slice(g * HALF, (g + 1) * HALF)
             nc.tensor.matmul_mx(
-                out=h_ps[c][:, t, :],
-                lhsT=w1_codes[s][:, (ts or t) * P : ((ts or t) + 1) * P].bitcast(FP8X4),
-                lhsT_scale=w1_scales[s][:, (ts or t) * P : ((ts or t) + 1) * P],
-                rhs=x_codes[s][:, c * CH : (c + 1) * CH].bitcast(FP8X4),
-                rhs_scale=x_scales[PACK * s :, c * CH : (c + 1) * CH],
-                start=start,
-                stop=stop,
+                out=h_ps[t][g][:],
+                lhsT=w1_codes[s][:, cols].bitcast(FP8X4),
+                lhsT_scale=w1_scales[s][:, cols],
+                rhs=x_codes[s][:, tokens].bitcast(FP8X4),
+                rhs_scale=x_scales[PACK * s :, tokens],
+                start=(s == 0),
+                stop=(s == PASSES - 1),
             )
+
+        def first_layer_pass(s):
+            for g in range(2):
+                for t in range(PACK):
+                    first_layer(s, t, g)
 
         vec, act = nc.vector.tensor_copy, nc.scalar.copy
 
@@ -128,14 +131,12 @@ def tile_picked_sub_mlp_relu_sub_e_kernel(tc, xT, w1, w2, gate, offs, pos1, pos2
         nc.sync.dma_start(offs_sb[:], offs)
         load_x(0, x_cuts[0][1])
         load_x(0, x_cuts[0][2])
-        load_w1(0, w1_cuts[0][0])
-        load_x(1, x_cuts[1][0])
-        load_x(1, x_cuts[1][1])
-        load_x(2, x_cuts[2][0])
-        load_x(2, x_cuts[2][1])
-        load_w1(1, w1_cuts[1][0])
-        load_w1(2, w1_cuts[2][0])
-        load_w1(2, w1_cuts[2][1])
+        for s in (1, 2):
+            for cut in x_cuts[s]:
+                load_x(s, cut)
+        for s in range(PASSES):
+            for cut in w1_cuts[s]:
+                load_w1(s, cut)
         for cut in w2_cuts:
             nc.sync.dma_start(out=w2_raw[cut][:], in_=w2[:, cut[0] : cut[1]].rearrange("(p j) n -> p j n", j=PACK))
         for d, pos in enumerate((pos1, pos2, pos3)):
@@ -143,50 +144,68 @@ def tile_picked_sub_mlp_relu_sub_e_kernel(tc, xT, w1, w2, gate, offs, pos1, pos2
         for m in range(NB):
             nc.sync.dma_start(out=gate_sb[m][:], in_=gate[:, m * P : (m + 1) * P, :].rearrange("d p v -> p d v"))
 
-        def do_w1(s, copy):
-            group_w1(copy, s, w1_cuts[s][0])
-            quantize(w1_codes[s], w1_scales[s], w1_grp[s], 0, H)
-
-        do_x(0, x_cuts[0][0], 0.5)
-        do_x(0, x_cuts[0][1], 0.5)
-        do_x(0, x_cuts[0][2], 0.45)
-        pick_words(0, 0, NCH)
-        do_w1(0, act)
-        do_x(1, x_cuts[1][0], 0.4)
-        do_x(1, x_cuts[1][1], 0.6)
-        pick_words(1, 0, NCH)
-        do_x(2, x_cuts[2][0], 0.6)
+        do_x(0, x_cuts[0][0], 0.4)
+        do_x(0, x_cuts[0][1], 0.6)
+        do_x(0, x_cuts[0][2], 0.6)
+        pick_words(0)
+        do_x(1, x_cuts[1][0], 0.9)
+        do_x(1, x_cuts[1][1], 0.75)
+        pick_words(1)
+        do_x(2, x_cuts[2][0], 0.85)
         do_x(2, x_cuts[2][1], 0.5)
-        for c in range(NCH):
-            pick_bytes(c, c + 1)
-            pick_words(2, c, c + 1)
+        nc.vector.tensor_copy(x_scales[:], x_all_sc[:].indirect(offs_sb[:]))
         for b in range(WARM):
-            first_layer(0, b % NCH, 0, True, True, ts=1 + b % 3)
-        for c in range(NCH):
-            first_layer(0, c, 0, True, False)
-        do_w1(1, act)
-        for c in range(NCH):
-            first_layer(1, c, 0, False, False)
-        group_w1(act, 2, w1_cuts[2][0])
-        group_w1(vec, 2, w1_cuts[2][1])
+            rows = slice((b % PACK) * P, (b % PACK + 1) * P)
+            nc.tensor.matmul_mx(
+                out=h_ps[b % PACK][b // PACK][:],
+                lhsT=x_codes[0][:, rows].bitcast(FP8X4),
+                lhsT_scale=x_scales[:, rows],
+                rhs=x_codes[1][:, :HALF].bitcast(FP8X4),
+                rhs_scale=x_scales[PACK:, :HALF],
+                start=True,
+                stop=True,
+            )
+        group_w1(act, 0, w1_cuts[0][0], 0, 4)
+        quantize(w1_codes[0], w1_scales[0], w1_grp[0], 0, H)
+        first_layer_pass(0)
+        group_w1(act, 1, w1_cuts[1][0], 0, 2)
+        group_w1(vec, 1, w1_cuts[1][0], 2, 4)
+        pick_words(2)
+        quantize(w1_codes[1], w1_scales[1], w1_grp[1], 0, H)
+        first_layer_pass(1)
+        group_w1(act, 2, w1_cuts[2][0], 0, 4)
+        group_w1(act, 2, w1_cuts[2][1], 0, 2)
+        group_w1(vec, 2, w1_cuts[2][1], 2, 4)
         for t in range(PACK):
             quantize(w1_codes[2], w1_scales[2], w1_grp[2], t * P, (t + 1) * P)
-        group(vec, w2_grp, 0, w2_raw[w2_cuts[0]], 0, N // 2)
-        for c in range(NCH):
-            first_layer(2, c, 0, False, True)
-            for t in range(1, PACK):
-                for s in range(PASSES):
-                    first_layer(s, c, t, s == 0, s == PASSES - 1)
-            nc.scalar.activation(h_grp[c][:].rearrange("p (n t) -> p n t", t=PACK), h_ps[c][:].rearrange("p t n -> p n t"), RELU)
-            if c == 0:
-                group(vec, w2_grp, N // 2, w2_raw[w2_cuts[1]], 0, N // 2)
-                quantize(w2_codes, w2_scales, w2_grp, 0, N)
+        first_layer_pass(2)
+        w2_grp = [tile([P, PACK * P], BF16, "w2_grp0")]
+        group(act, w2_grp[0], 0, w2_raw[w2_cuts[0]], 0, P)
+        for g in range(2):
+            for t in range(PACK):
+                if t % 2 == 0:
+                    nc.scalar.activation(h_lin[g][:, t, :], h_ps[t][g][:], RELU)
+                else:
+                    nc.vector.tensor_scalar_max(h_lin[g][:, t, :], h_ps[t][g][:], 0.0)
+        for g in range(2):
+            group(act, h_grp[g], 0, h_lin[g], 0, 96)
+            group(vec, h_grp[g], 0, h_lin[g], 96, HALF)
             nc.vector.quantize_mx(
-                out=h_codes[:, c * CH : (c + 1) * CH].bitcast(FP8X4), scales=h_scales[:, c * CH : (c + 1) * CH], in_=h_grp[c][:]
+                out=h_codes[:, g * HALF : (g + 1) * HALF].bitcast(FP8X4),
+                scales=h_scales[:, g * HALF : (g + 1) * HALF],
+                in_=h_grp[g][:],
             )
+            if g == 0:
+                quantize_w2(0)
+        for m, tag in ((1, "h_lin0"), (2, "h_lin1"), (3, "h_grp0")):
+            w2_grp.append(keep.tile([P, PACK * P], BF16, name="w2_grp%d" % m, tag=tag, align_bytes=64))
+        group(act, w2_grp[1], -P, w2_raw[w2_cuts[0]], P, N // 2)
+        group(vec, w2_grp[2], 0, w2_raw[w2_cuts[1]], 0, P)
+        quantize_w2(1)
+        quantize_w2(2)
 
-        y_ps = [psum.tile([P, S], F32, name="y_ps%d" % m) for m in range(NB)]
-        y_ps_late = psum.tile([P, S], F32, name="y_ps_late", tag="h_ps0")
+        banks = ((0, 0), (1, 0), (2, 0), (3, 0), (0, 1), (1, 1))
+        y_ps = [psum.tile([P, S], F32, name="y_ps%d" % b, tag="h_ps%d%d" % banks[b]) for b in range(6)]
 
         def second_layer(bank, m, n0, n1):
             cols = slice(m * P, (m + 1) * P)
@@ -200,13 +219,17 @@ def tile_picked_sub_mlp_relu_sub_e_kernel(tc, xT, w1, w2, gate, offs, pos1, pos2
                 stop=True,
             )
 
-        second_layer(y_ps[0], 0, 0, S // 2)
-        nc.scalar.copy(y_sb[0][:, : S // 2], y_ps[0][:, : S // 2])
-        second_layer(y_ps_late, 0, S // 2, S)
-        nc.scalar.copy(y_sb[0][:, S // 2 :], y_ps_late[:, S // 2 :])
+        second_layer(y_ps[0], 0, 0, HALF)
+        nc.scalar.copy(y_sb[0][:, :HALF], y_ps[0][:, :HALF])
+        second_layer(y_ps[1], 0, HALF, HALF + P)
+        second_layer(y_ps[2], 0, HALF + P, S)
+        nc.scalar.copy(y_sb[0][:, HALF : HALF + P], y_ps[1][:, HALF : HALF + P])
+        nc.vector.tensor_copy(y_sb[0][:, HALF + P :], y_ps[2][:, HALF + P :])
+        group(act, w2_grp[3], -P, w2_raw[w2_cuts[1]], P, N // 2)
+        quantize_w2(3)
         for m in range(1, NB):
-            second_layer(y_ps[m], m, 0, S)
-            nc.scalar.copy(y_sb[m][:], y_ps[m][:])
+            second_layer(y_ps[m + 2], m, 0, S)
+            nc.scalar.copy(y_sb[m][:], y_ps[m + 2][:])
 
         def add_parts(m):
             nc.vector.tensor_tensor(part[m][:], prod[m][0][:], prod[m][1][:], ADD)

@@ -34,7 +34,7 @@ def tile_picked_sub_mlp_relu_sub_e_kernel(tc, xT, w1, w2, gate, offs, pos1, pos2
 
         offs_sb = tile([P, S // 16], U16, "offs_sb")
         pos_sb = [tile([P, V // 16], U16, "pos_sb%d" % d) for d in range(D)]
-        x_cuts = (((0, 256), (256, 512), (512, T)), ((0, 512), (512, T)), ((0, 512), (512, T)))
+        x_cuts = (((0, T),), ((0, T),), ((0, T // 2), (T // 2, T)))
         x_raw = {
             (s, cut): tile([P, PACK, cut[1] - cut[0]], F32, "x_raw%d_%d" % (s, cut[0])) for s in range(PASSES) for cut in x_cuts[s]
         }
@@ -43,15 +43,11 @@ def tile_picked_sub_mlp_relu_sub_e_kernel(tc, xT, w1, w2, gate, offs, pos1, pos2
         x_all_sc = tile([P, T], U8, "x_all_sc")
         x_codes = [tile([P, S], U32, "x_codes%d" % s) for s in range(PASSES)]
         x_scales = tile([P, S], U8, "x_scales")
-        w1_cuts = ((0, H),), ((0, H),), ((0, H // 2), (H // 2, H))
-        w1_raw = {
-            (s, cut): tile([P, PACK, cut[1] - cut[0]], F32, "w1_raw%d_%d" % (s, cut[0])) for s in range(PASSES) for cut in w1_cuts[s]
-        }
+        w1_raw = [tile([P, PACK, H], F32, "w1_raw%d" % s) for s in range(PASSES)]
         w1_grp = [tile([P, PACK * H], BF16, "w1_grp%d" % s) for s in range(PASSES)]
         w1_codes = [tile([P, H], U32, "w1_codes%d" % s) for s in range(PASSES)]
         w1_scales = [tile([P, H], U8, "w1_scales%d" % s) for s in range(PASSES)]
-        w2_cuts = ((0, N // 2), (N // 2, N))
-        w2_raw = {cut: tile([P, PACK, N // 2], F32, "w2_raw%d" % cut[0]) for cut in w2_cuts}
+        w2_raw = tile([P, PACK, N], F32, "w2_raw")
         w2_codes = tile([P, N], U32, "w2_codes")
         w2_scales = tile([P, N], U8, "w2_scales")
         h_lin = [tile([P, PACK, HALF], BF16, "h_lin%d" % g) for g in range(2)]
@@ -67,22 +63,22 @@ def tile_picked_sub_mlp_relu_sub_e_kernel(tc, xT, w1, w2, gate, offs, pos1, pos2
 
         def load_x(s, cut):
             rows = xT[s * KP : (s + 1) * KP, cut[0] : cut[1]].rearrange("(p j) t -> p j t", j=PACK)
-            nc.sync.dma_start(out=x_raw[s, cut][:], in_=rows)
+            if cut == (0, T):
+                nc.sync.dma_start(out=x_raw[s, cut][:, 0:2, :], in_=rows[:, 0:2, :])
+                nc.sync.dma_start(out=x_raw[s, cut][:, 2:4, :], in_=rows[:, 2:4, :])
+            else:
+                nc.sync.dma_start(out=x_raw[s, cut][:], in_=rows)
 
-        def load_w1(s, cut):
-            rows = w1[s * KP : (s + 1) * KP, cut[0] : cut[1]].rearrange("(p j) h -> p j h", j=PACK)
-            nc.sync.dma_start(out=w1_raw[s, cut][:], in_=rows)
-
-        def group(copy, grp, g0, raw, r0, r1):
+        def group(copy, grp, g0, raw, r0, r1, j0=0, j1=PACK):
             copy(
-                out=grp[:, PACK * (g0 + r0) : PACK * (g0 + r1)].rearrange("p (c i j) -> p c j i", i=4, j=PACK),
-                in_=raw[:, :, r0:r1].rearrange("p j (c i) -> p c j i", i=4),
+                out=grp[:, PACK * (g0 + r0) : PACK * (g0 + r1)].rearrange("p (c i j) -> p c j i", i=4, j=PACK)[:, :, j0:j1],
+                in_=raw[:, j0:j1, r0:r1].rearrange("p j (c i) -> p c j i", i=4),
             )
 
-        def group_w1(copy, s, cut, t0, t1):
+        def group_w1(copy, s, t0, t1):
             copy(
-                out=w1_grp[s][:].rearrange("p (t m j) -> p m j t", t=4, j=PACK)[:, cut[0] // 4 : cut[1] // 4, :, t0:t1],
-                in_=w1_raw[s, cut][:].rearrange("p j (m t) -> p m j t", t=4)[:, :, :, t0:t1],
+                out=w1_grp[s][:].rearrange("p (t m j) -> p m j t", t=4, j=PACK)[:, :, :, t0:t1],
+                in_=w1_raw[s][:].rearrange("p j (m t) -> p m j t", t=4)[:, :, :, t0:t1],
             )
 
         def quantize_w2(m):
@@ -95,17 +91,16 @@ def tile_picked_sub_mlp_relu_sub_e_kernel(tc, xT, w1, w2, gate, offs, pos1, pos2
                 out=codes[:, n0:n1].bitcast(FP8X4), scales=scales[:, n0:n1], in_=grouped[:, PACK * n0 : PACK * n1]
             )
 
-        def do_x(s, cut, share):
-            width = cut[1] - cut[0]
-            n_act = int(width * share) // 8 * 8
-            if n_act:
-                group(act, x_grp[s], cut[0], x_raw[s, cut], 0, n_act)
-            if n_act < width:
-                group(vec, x_grp[s], cut[0], x_raw[s, cut], n_act, width)
-            quantize(x_all[s], x_all_sc[PACK * s :, :], x_grp[s], cut[0], cut[1])
+        def do_x(s, cut, t0, t1, share):
+            split = t0 + int((t1 - t0) * share) // 8 * 8
+            if split > t0:
+                group(act, x_grp[s], cut[0], x_raw[s, cut], t0, split)
+            if split < t1:
+                group(vec, x_grp[s], cut[0], x_raw[s, cut], split, t1)
+            quantize(x_all[s], x_all_sc[PACK * s :, :], x_grp[s], cut[0] + t0, cut[0] + t1)
 
-        def pick_words(s):
-            nc.vector.tensor_copy(x_codes[s][:], x_all[s][:].indirect(offs_sb[:]))
+        def pick_words(s, n0, n1):
+            nc.vector.tensor_copy(x_codes[s][:, n0:n1], x_all[s][:].indirect(offs_sb[:, n0 // 16 : n1 // 16]))
 
         def first_layer(s, t, g):
             cols = slice(t * P, (t + 1) * P)
@@ -122,37 +117,36 @@ def tile_picked_sub_mlp_relu_sub_e_kernel(tc, xT, w1, w2, gate, offs, pos1, pos2
 
         def first_layer_pass(s):
             for g in range(2):
-                for t in range(PACK):
+                for t in (2, 3, 0, 1):
                     first_layer(s, t, g)
 
         vec, act = nc.vector.tensor_copy, nc.scalar.copy
 
-        load_x(0, x_cuts[0][0])
+        load_x(0, (0, T))
         nc.sync.dma_start(offs_sb[:], offs)
-        load_x(0, x_cuts[0][1])
-        load_x(0, x_cuts[0][2])
-        for s in (1, 2):
-            for cut in x_cuts[s]:
-                load_x(s, cut)
+        load_x(1, (0, T))
+        for cut in x_cuts[2]:
+            load_x(2, cut)
         for s in range(PASSES):
-            for cut in w1_cuts[s]:
-                load_w1(s, cut)
-        for cut in w2_cuts:
-            nc.sync.dma_start(out=w2_raw[cut][:], in_=w2[:, cut[0] : cut[1]].rearrange("(p j) n -> p j n", j=PACK))
+            nc.sync.dma_start(out=w1_raw[s][:], in_=w1[s * KP : (s + 1) * KP, :].rearrange("(p j) h -> p j h", j=PACK))
+        nc.sync.dma_start(out=w2_raw[:], in_=w2.rearrange("(p j) n -> p j n", j=PACK))
         for d, pos in enumerate((pos1, pos2, pos3)):
             nc.sync.dma_start(pos_sb[d][:], pos)
         for m in range(NB):
             nc.sync.dma_start(out=gate_sb[m][:], in_=gate[:, m * P : (m + 1) * P, :].rearrange("d p v -> p d v"))
 
-        do_x(0, x_cuts[0][0], 0.4)
-        do_x(0, x_cuts[0][1], 0.6)
-        do_x(0, x_cuts[0][2], 0.6)
-        pick_words(0)
-        do_x(1, x_cuts[1][0], 0.9)
-        do_x(1, x_cuts[1][1], 0.75)
-        pick_words(1)
-        do_x(2, x_cuts[2][0], 0.85)
-        do_x(2, x_cuts[2][1], 0.5)
+        group(act, x_grp[0], 0, x_raw[0, (0, T)], 0, 576, 0, 2)
+        group(vec, x_grp[0], 0, x_raw[0, (0, T)], 576, T, 0, 2)
+        group(vec, x_grp[0], 0, x_raw[0, (0, T)], 0, T // 2, 2, 4)
+        group(act, x_grp[0], 0, x_raw[0, (0, T)], T // 2, T, 2, 4)
+        for n0 in (0, T // 2):
+            quantize(x_all[0], x_all_sc, x_grp[0], n0, n0 + T // 2)
+        pick_words(0, 0, S)
+        do_x(1, (0, T), 0, T // 2, 0.4)
+        do_x(1, (0, T), T // 2, T, 0.6)
+        pick_words(1, 0, S)
+        do_x(2, x_cuts[2][0], 0, T // 2, 0.8)
+        do_x(2, x_cuts[2][1], 0, T // 2, 0.55)
         nc.vector.tensor_copy(x_scales[:], x_all_sc[:].indirect(offs_sb[:]))
         for b in range(WARM):
             rows = slice((b % PACK) * P, (b % PACK + 1) * P)
@@ -165,24 +159,24 @@ def tile_picked_sub_mlp_relu_sub_e_kernel(tc, xT, w1, w2, gate, offs, pos1, pos2
                 start=True,
                 stop=True,
             )
-        group_w1(act, 0, w1_cuts[0][0], 0, 4)
+        group_w1(act, 0, 0, 4)
         quantize(w1_codes[0], w1_scales[0], w1_grp[0], 0, H)
         first_layer_pass(0)
-        group_w1(act, 1, w1_cuts[1][0], 0, 2)
-        group_w1(vec, 1, w1_cuts[1][0], 2, 4)
-        pick_words(2)
+        pick_words(2, 0, HALF)
+        group_w1(act, 1, 0, 2)
+        group_w1(vec, 1, 2, 4)
         quantize(w1_codes[1], w1_scales[1], w1_grp[1], 0, H)
         first_layer_pass(1)
-        group_w1(act, 2, w1_cuts[2][0], 0, 4)
-        group_w1(act, 2, w1_cuts[2][1], 0, 2)
-        group_w1(vec, 2, w1_cuts[2][1], 2, 4)
-        for t in range(PACK):
+        group_w1(act, 2, 0, 2)
+        group_w1(vec, 2, 2, 4)
+        for t in (2, 3, 0, 1):
             quantize(w1_codes[2], w1_scales[2], w1_grp[2], t * P, (t + 1) * P)
+        pick_words(2, HALF, S)
         first_layer_pass(2)
         w2_grp = [tile([P, PACK * P], BF16, "w2_grp0")]
-        group(act, w2_grp[0], 0, w2_raw[w2_cuts[0]], 0, P)
+        group(act, w2_grp[0], 0, w2_raw, 0, P)
         for g in range(2):
-            for t in range(PACK):
+            for t in (2, 3, 0, 1):
                 if t % 2 == 0:
                     nc.scalar.activation(h_lin[g][:, t, :], h_ps[t][g][:], RELU)
                 else:
@@ -199,8 +193,8 @@ def tile_picked_sub_mlp_relu_sub_e_kernel(tc, xT, w1, w2, gate, offs, pos1, pos2
                 quantize_w2(0)
         for m, tag in ((1, "h_lin0"), (2, "h_lin1"), (3, "h_grp0")):
             w2_grp.append(keep.tile([P, PACK * P], BF16, name="w2_grp%d" % m, tag=tag, align_bytes=64))
-        group(act, w2_grp[1], -P, w2_raw[w2_cuts[0]], P, N // 2)
-        group(vec, w2_grp[2], 0, w2_raw[w2_cuts[1]], 0, P)
+        group(act, w2_grp[1], -P, w2_raw, P, 2 * P)
+        group(vec, w2_grp[2], -2 * P, w2_raw, 2 * P, 3 * P)
         quantize_w2(1)
         quantize_w2(2)
 
@@ -225,7 +219,7 @@ def tile_picked_sub_mlp_relu_sub_e_kernel(tc, xT, w1, w2, gate, offs, pos1, pos2
         second_layer(y_ps[2], 0, HALF + P, S)
         nc.scalar.copy(y_sb[0][:, HALF : HALF + P], y_ps[1][:, HALF : HALF + P])
         nc.vector.tensor_copy(y_sb[0][:, HALF + P :], y_ps[2][:, HALF + P :])
-        group(act, w2_grp[3], -P, w2_raw[w2_cuts[1]], P, N // 2)
+        group(act, w2_grp[3], -3 * P, w2_raw, 3 * P, N)
         quantize_w2(3)
         for m in range(1, NB):
             second_layer(y_ps[m + 2], m, 0, S)

from contextlib import ExitStack

import concourse.mybir as mybir

K, T, D, S, V, H, N = 1536, 1024, 3, 512, 256, 512, 512
P = 128
PACK = 4
KP = P * PACK
PASSES = K // KP
NB = N // P
HALF = S // 2
WARM = 6
FLOPS = 2 * S * H * (K + N) + 5 * N * V

F32 = mybir.dt.float32
BF16 = mybir.dt.bfloat16
U32 = mybir.dt.uint32
U16 = mybir.dt.uint16
U8 = mybir.dt.uint8
FP8X4 = mybir.dt.float8_e4m3fn_x4
RELU = mybir.ActivationFunctionType.Relu
MULT = mybir.AluOpType.mult
ADD = mybir.AluOpType.add


def tile_picked_sub_mlp_relu_sub_e_kernel(tc, xT, w1, w2, gate, offs, pos1, pos2, pos3, out):
    nc = tc.nc
    with ExitStack() as ctx:
        keep = ctx.enter_context(tc.tile_pool(name="keep", bufs=1))
        psum = ctx.enter_context(tc.psum_pool(name="psum", bufs=1))

        def tile(shape, dtype, name):
            return keep.tile(shape, dtype, name=name, align_bytes=64)

        offs_sb = tile([P, S // 16], U16, "offs_sb")
        pos_sb = [tile([P, V // 16], U16, "pos_sb%d" % d) for d in range(D)]
        x_cuts = (((0, T),), ((0, T),), ((0, T // 2), (T // 2, T)))
        x_raw = {
            (s, cut): tile([P, PACK, cut[1] - cut[0]], F32, "x_raw%d_%d" % (s, cut[0])) for s in range(PASSES) for cut in x_cuts[s]
        }
        x_grp = [tile([P, PACK * T], BF16, "x_grp%d" % s) for s in range(PASSES)]
        x_all = [tile([P, T], U32, "x_all%d" % s) for s in range(PASSES)]
        x_all_sc = tile([P, T], U8, "x_all_sc")
        x_codes = [tile([P, S], U32, "x_codes%d" % s) for s in range(PASSES)]
        x_scales = tile([P, S], U8, "x_scales")
        w1_raw = [tile([P, PACK, H], F32, "w1_raw%d" % s) for s in range(PASSES)]
        w1_grp = [tile([P, PACK * H], BF16, "w1_grp%d" % s) for s in range(PASSES)]
        w1_codes = [tile([P, H], U32, "w1_codes%d" % s) for s in range(PASSES)]
        w1_scales = [tile([P, H], U8, "w1_scales%d" % s) for s in range(PASSES)]
        w2_raw = tile([P, PACK, N], F32, "w2_raw")
        w2_codes = tile([P, N], U32, "w2_codes")
        w2_scales = tile([P, N], U8, "w2_scales")
        h_lin = [tile([P, PACK, HALF], BF16, "h_lin%d" % g) for g in range(2)]
        h_grp = [tile([P, PACK * HALF], BF16, "h_grp%d" % g) for g in range(2)]
        h_codes = tile([P, S], U32, "h_codes")
        h_scales = tile([P, S], U8, "h_scales")
        y_sb = [tile([P, S], F32, "y_sb%d" % m) for m in range(NB)]
        gate_sb = [tile([P, D, V], F32, "gate_sb%d" % m) for m in range(NB)]
        prod = [[tile([P, V], F32, "prod%d%d" % (m, d)) for d in range(D)] for m in range(NB)]
        part = [tile([P, V], F32, "part%d" % m) for m in range(NB)]
        res = [tile([P, V], F32, "res%d" % m) for m in range(NB)]
        h_ps = [[psum.tile([P, HALF], F32, name="h_ps%d%d" % (t, g)) for g in range(2)] for t in range(PACK)]

        def load_x(s, cut):
            rows = xT[s * KP : (s + 1) * KP, cut[0] : cut[1]].rearrange("(p j) t -> p j t", j=PACK)
            if cut == (0, T):
                nc.sync.dma_start(out=x_raw[s, cut][:, 0:2, :], in_=rows[:, 0:2, :])
                nc.sync.dma_start(out=x_raw[s, cut][:, 2:4, :], in_=rows[:, 2:4, :])
            else:
                nc.sync.dma_start(out=x_raw[s, cut][:], in_=rows)

        def group(copy, grp, g0, raw, r0, r1, j0=0, j1=PACK):
            copy(
                out=grp[:, PACK * (g0 + r0) : PACK * (g0 + r1)].rearrange("p (c i j) -> p c j i", i=4, j=PACK)[:, :, j0:j1],
                in_=raw[:, j0:j1, r0:r1].rearrange("p j (c i) -> p c j i", i=4),
            )

        def group_w1(copy, s, t0, t1):
            copy(
                out=w1_grp[s][:].rearrange("p (t m j) -> p m j t", t=4, j=PACK)[:, :, :, t0:t1],
                in_=w1_raw[s][:].rearrange("p j (m t) -> p m j t", t=4)[:, :, :, t0:t1],
            )

        def quantize_w2(m):
            nc.vector.quantize_mx(
                out=w2_codes[:, m * P : (m + 1) * P].bitcast(FP8X4), scales=w2_scales[:, m * P : (m + 1) * P], in_=w2_grp[m][:]
            )

        def quantize(codes, scales, grouped, n0, n1):
            nc.vector.quantize_mx(
                out=codes[:, n0:n1].bitcast(FP8X4), scales=scales[:, n0:n1], in_=grouped[:, PACK * n0 : PACK * n1]
            )

        def do_x(s, cut, t0, t1, share):
            split = t0 + int((t1 - t0) * share) // 8 * 8
            if split > t0:
                group(act, x_grp[s], cut[0], x_raw[s, cut], t0, split)
            if split < t1:
                group(vec, x_grp[s], cut[0], x_raw[s, cut], split, t1)
            quantize(x_all[s], x_all_sc[PACK * s :, :], x_grp[s], cut[0] + t0, cut[0] + t1)

        def pick_words(s, n0, n1):
            nc.vector.tensor_copy(x_codes[s][:, n0:n1], x_all[s][:].indirect(offs_sb[:, n0 // 16 : n1 // 16]))

        def first_layer(s, t, g):
            cols = slice(t * P, (t + 1) * P)
            tokens = slice(g * HALF, (g + 1) * HALF)
            nc.tensor.matmul_mx(
                out=h_ps[t][g][:],
                lhsT=w1_codes[s][:, cols].bitcast(FP8X4),
                lhsT_scale=w1_scales[s][:, cols],
                rhs=x_codes[s][:, tokens].bitcast(FP8X4),
                rhs_scale=x_scales[PACK * s :, tokens],
                start=(s == 0),
                stop=(s == PASSES - 1),
            )

        def first_layer_pass(s):
            for g in range(2):
                for t in (2, 3, 0, 1):
                    first_layer(s, t, g)

        vec, act = nc.vector.tensor_copy, nc.scalar.copy

        load_x(0, (0, T))
        nc.sync.dma_start(offs_sb[:], offs)
        load_x(1, (0, T))
        for cut in x_cuts[2]:
            load_x(2, cut)
        for s in range(PASSES):
            nc.sync.dma_start(out=w1_raw[s][:], in_=w1[s * KP : (s + 1) * KP, :].rearrange("(p j) h -> p j h", j=PACK))
        nc.sync.dma_start(out=w2_raw[:], in_=w2.rearrange("(p j) n -> p j n", j=PACK))
        for d, pos in enumerate((pos1, pos2, pos3)):
            nc.sync.dma_start(pos_sb[d][:], pos)
        for m in range(NB):
            nc.sync.dma_start(out=gate_sb[m][:], in_=gate[:, m * P : (m + 1) * P, :].rearrange("d p v -> p d v"))

        group(act, x_grp[0], 0, x_raw[0, (0, T)], 0, 576, 0, 2)
        group(vec, x_grp[0], 0, x_raw[0, (0, T)], 576, T, 0, 2)
        group(vec, x_grp[0], 0, x_raw[0, (0, T)], 0, T // 2, 2, 4)
        group(act, x_grp[0], 0, x_raw[0, (0, T)], T // 2, T, 2, 4)
        for n0 in (0, T // 2):
            quantize(x_all[0], x_all_sc, x_grp[0], n0, n0 + T // 2)
        pick_words(0, 0, S)
        do_x(1, (0, T), 0, T // 2, 0.4)
        do_x(1, (0, T), T // 2, T, 0.6)
        pick_words(1, 0, S)
        do_x(2, x_cuts[2][0], 0, T // 2, 0.8)
        do_x(2, x_cuts[2][1], 0, T // 2, 0.55)
        nc.vector.tensor_copy(x_scales[:], x_all_sc[:].indirect(offs_sb[:]))
        for b in range(WARM):
            rows = slice((b % PACK) * P, (b % PACK + 1) * P)
            nc.tensor.matmul_mx(
                out=h_ps[b % PACK][b // PACK][:],
                lhsT=x_codes[0][:, rows].bitcast(FP8X4),
                lhsT_scale=x_scales[:, rows],
                rhs=x_codes[1][:, :HALF].bitcast(FP8X4),
                rhs_scale=x_scales[PACK:, :HALF],
                start=True,
                stop=True,
            )
        group_w1(act, 0, 0, 4)
        quantize(w1_codes[0], w1_scales[0], w1_grp[0], 0, H)
        first_layer_pass(0)
        pick_words(2, 0, HALF)
        group_w1(act, 1, 0, 2)
        group_w1(vec, 1, 2, 4)
        quantize(w1_codes[1], w1_scales[1], w1_grp[1], 0, H)
        first_layer_pass(1)
        group_w1(act, 2, 0, 2)
        group_w1(vec, 2, 2, 4)
        for t in (2, 3, 0, 1):
            quantize(w1_codes[2], w1_scales[2], w1_grp[2], t * P, (t + 1) * P)
        pick_words(2, HALF, S)
        first_layer_pass(2)
        w2_grp = [tile([P, PACK * P], BF16, "w2_grp0")]
        group(act, w2_grp[0], 0, w2_raw, 0, P)
        for g in range(2):
            for t in (2, 3, 0, 1):
                if t % 2 == 0:
                    nc.scalar.activation(h_lin[g][:, t, :], h_ps[t][g][:], RELU)
                else:
                    nc.vector.tensor_scalar_max(h_lin[g][:, t, :], h_ps[t][g][:], 0.0)
        for g in range(2):
            group(act, h_grp[g], 0, h_lin[g], 0, 96)
            group(vec, h_grp[g], 0, h_lin[g], 96, HALF)
            nc.vector.quantize_mx(
                out=h_codes[:, g * HALF : (g + 1) * HALF].bitcast(FP8X4),
                scales=h_scales[:, g * HALF : (g + 1) * HALF],
                in_=h_grp[g][:],
            )
            if g == 0:
                quantize_w2(0)
        for m, tag in ((1, "h_lin0"), (2, "h_lin1"), (3, "h_grp0")):
            w2_grp.append(keep.tile([P, PACK * P], BF16, name="w2_grp%d" % m, tag=tag, align_bytes=64))
        group(act, w2_grp[1], -P, w2_raw, P, 2 * P)
        group(vec, w2_grp[2], -2 * P, w2_raw, 2 * P, 3 * P)
        quantize_w2(1)
        quantize_w2(2)

        banks = ((0, 0), (1, 0), (2, 0), (3, 0), (0, 1), (1, 1))
        y_ps = [psum.tile([P, S], F32, name="y_ps%d" % b, tag="h_ps%d%d" % banks[b]) for b in range(6)]

        def second_layer(bank, m, n0, n1):
            cols = slice(m * P, (m + 1) * P)
            nc.tensor.matmul_mx(
                out=bank[:, n0:n1],
                lhsT=w2_codes[:, cols].bitcast(FP8X4),
                lhsT_scale=w2_scales[:, cols],
                rhs=h_codes[:, n0:n1].bitcast(FP8X4),
                rhs_scale=h_scales[:, n0:n1],
                start=True,
                stop=True,
            )

        second_layer(y_ps[0], 0, 0, HALF)
        nc.scalar.copy(y_sb[0][:, :HALF], y_ps[0][:, :HALF])
        second_layer(y_ps[1], 0, HALF, HALF + P)
        second_layer(y_ps[2], 0, HALF + P, S)
        nc.scalar.copy(y_sb[0][:, HALF : HALF + P], y_ps[1][:, HALF : HALF + P])
        nc.vector.tensor_copy(y_sb[0][:, HALF + P :], y_ps[2][:, HALF + P :])
        group(act, w2_grp[3], -3 * P, w2_raw, 3 * P, N)
        quantize_w2(3)
        for m in range(1, NB):
            second_layer(y_ps[m + 2], m, 0, S)
            nc.scalar.copy(y_sb[m][:], y_ps[m + 2][:])

        def add_parts(m):
            nc.vector.tensor_tensor(part[m][:], prod[m][0][:], prod[m][1][:], ADD)

        def add_last(m):
            nc.vector.tensor_tensor(res[m][:], part[m][:], prod[m][2][:], ADD)
            nc.sync.dma_start(out=out[m * P : (m + 1) * P, :], in_=res[m][:])

        for m in range(NB):
            for d in range(D):
                nc.vector.tensor_tensor(prod[m][d][:], y_sb[m][:].indirect(pos_sb[d][:]), gate_sb[m][:, d, :], MULT)
                if m and d == 0:
                    add_last(m - 1)
                if d == 2:
                    add_parts(m)
        add_last(NB - 1)
